import numpy as np
import ml_dtypes


def mxq(x, axis, fmt="e4m3"):
    dtype, down = {"e4m3": (ml_dtypes.float8_e4m3fn, 7), "e5m2": (ml_dtypes.float8_e5m2, 14)}[fmt]
    v = np.moveaxis(np.asarray(x, np.float32).astype(ml_dtypes.bfloat16).astype(np.float64), axis, -1)
    blocks = v.reshape(v.shape[:-1] + (-1, 32))
    amax = np.abs(blocks).max(-1, keepdims=True)
    byte = np.maximum(np.where(amax > 0, np.frexp(amax)[1] - 1 + 127, 0) - down, 1)
    scale = np.exp2(byte - 127.0)
    codes = (blocks / scale).astype(np.float32).astype(dtype).astype(np.float64)
    return np.moveaxis((codes * scale).reshape(v.shape), -1, axis)


WIDE = False


def mx_kscale(k):
    if not WIDE:
        return np.ones(k)
    levels = np.array([10, -10, 5, -5, 0])
    if k % 512:
        return np.exp2(np.random.permutation(np.resize(levels, k // 32))).repeat(32)
    a = np.empty((k // 512, 16))
    for p in range(k // 512):
        a[p, :8] = np.random.permutation(np.resize(levels, 8))
        for g in range(8):
            far = levels[np.abs(levels - a[p, g]) >= 10]
            a[p, g + 8] = far[np.random.randint(len(far))]
    return np.exp2(a.ravel()).repeat(32)


def f64(x):
    return np.asarray(x).astype(np.float64)


def striped(idx):
    return np.tile(np.asarray(idx).reshape(-1, 16).T, (8, 1)).astype(np.uint16)


def unstriped(offs):
    return offs[:16].T.reshape(-1).astype(np.int64)


E2M1 = np.array([0.0, 0.5, 1.0, 1.5, 2.0, 3.0, 4.0, 6.0, -0.0, -0.5, -1.0, -1.5, -2.0, -3.0, -4.0, -6.0])


def pack_weight(w, fmt):
    k, n = w.shape
    w = f64(np.asarray(w, np.float32).astype(ml_dtypes.bfloat16)).reshape(k // 32, 32, n)
    amax = np.abs(w).max(1)
    if fmt == "e4m3":
        byte = np.frexp(amax)[1] - 1 + 127 - 7
    else:
        mant, ex = np.frexp(amax / 6.0)
        byte = np.where(mant > 0.5, ex, ex - 1) + 127
    byte = np.clip(np.where(amax > 0, byte, 1), 1, 254)
    scaled = (w * np.exp2(127.0 - byte)[:, None, :]).reshape(k, n).astype(np.float32)
    by_word = np.ascontiguousarray(scaled.reshape(k // 512, 128, 4, n).transpose(0, 1, 3, 2))
    if fmt == "e4m3":
        words = by_word.astype(ml_dtypes.float8_e4m3fn).view(np.uint8)
    else:
        c = by_word.astype(ml_dtypes.float4_e2m1fn).view(np.uint8) & 0xF
        words = (c[..., 0::2] | (c[..., 1::2] << 4)).reshape(k // 512, 128, 2 * n)
    return np.ascontiguousarray(words), np.ascontiguousarray(byte.astype(np.uint8).reshape(k // 512, 16, n))


def unpack_weight(words, scales, fmt):
    g, _, n = scales.shape
    words = np.ascontiguousarray(words).reshape(g, 128, n, -1)
    if fmt == "e4m3":
        vals = words.view(ml_dtypes.float8_e4m3fn).astype(np.float64)
    else:
        nib = np.empty((g, 128, n, 4), np.uint8)
        nib[..., 0::2] = words & 0xF
        nib[..., 1::2] = words >> 4
        vals = E2M1[nib]
    vals = vals * np.repeat(np.exp2(scales.astype(np.float64) - 127.0), 8, axis=1)[..., None]
    return vals.transpose(0, 1, 3, 2).reshape(g * 512, n)


def bf(x):
    return np.asarray(x, np.float32).astype(ml_dtypes.bfloat16)


def planes(Y):
    r, m = Y.shape
    b = f64(bf(Y)).reshape(r // 32, 32, m)
    amax = np.abs(b).max(1)
    byte = np.clip(np.where(amax > 0, np.frexp(amax)[1] - 1 + 127 - 7, 1), 1, 254)
    codes = (b * np.exp2(127.0 - byte)[:, None, :]).reshape(r, m).astype(np.float32).astype(ml_dtypes.float8_e4m3fn).view(np.uint8)
    words = codes.reshape(r // 512, 128, 4, m).transpose(0, 1, 3, 2)
    return np.ascontiguousarray(words), np.ascontiguousarray(byte.astype(np.uint8).reshape(r // 512, 16, m))


K, T, J, I, N, M = 1024, 1024, 512, 512, 512, 512


def setup_inputs():
    n = np.random.standard_normal
    idx = np.random.permutation(T)[:J]
    idx2 = np.random.permutation(T)[:I]
    fk = mx_kscale(K)
    fn = mx_kscale(N)
    xqp = pack_weight(n((K, T)) / fk[:, None], "e2m1")
    wap = pack_weight(n((K, N)) * 1 / np.sqrt(K) * fk[:, None] * fn, "e4m3")
    wmp = pack_weight(n((N, M)) * 1 / np.sqrt(N) / fn[:, None], "e2m1")
    return {
        "xq_words": xqp[0],
        "xq_scales": xqp[1],
        "wa_words": wap[0],
        "wa_scales": wap[1],
        "res": (n((N, T)) * fn[:, None]).astype(np.float32),
        "wm_words": wmp[0],
        "wm_scales": wmp[1],
        "b": (np.random.uniform(-0.5, 0.5, (M, 1))).astype(np.float32),
        "offs": striped(idx),
        "offs2": striped(idx2),
    }


def reference(xq_words, xq_scales, wa_words, wa_scales, res, wm_words, wm_scales, b, offs, offs2):
    idx = unstriped(offs)
    idx2 = unstriped(offs2)
    xqu = unpack_weight(xq_words, xq_scales, "e2m1")
    wau = unpack_weight(wa_words, wa_scales, "e4m3")
    wmu = unpack_weight(wm_words, wm_scales, "e2m1")
    xqidxg = xqu[:, idx]
    p = wau.T @ xqidxg
    pg = np.zeros((N, T))
    pg[:, idx] = p
    up = f64(res) + pg
    us = up[:, idx2]
    usq = mxq(us, 0, "e4m3")
    z = wmu.T @ usq
    y = np.maximum(z + f64(b), 0.0)
    words, scales = planes(y)
    return y, words, scales

@@ -1,0 +1,205 @@
+from contextlib import ExitStack
+
+import concourse.mybir as mybir
+from concourse.masks import make_identity
+
+K, T, J, I, N, M = 1024, 1024, 512, 512, 512, 512
+FLOPS = 2 * K * N * J + 2 * N * M * I
+
+F32 = mybir.dt.float32
+BF16 = mybir.dt.bfloat16
+I32 = mybir.dt.int32
+U32 = mybir.dt.uint32
+U16 = mybir.dt.uint16
+U8 = mybir.dt.uint8
+FP8X4 = mybir.dt.float8_e4m3fn_x4
+FP4X4 = mybir.dt.float4_e2m1fn_x4
+ACT = mybir.ActivationFunctionType
+ALU = mybir.AluOpType
+
+P = 128
+PACK = 4
+PASSES = K // (P * PACK)
+BANK = 512
+HALF = 256
+
+
+def tile_list_second_reads_updated_page_pl_kernel(
+    tc, xq_words, xq_scales, wa_words, wa_scales, res, wm_words, wm_scales, b, offs, offs2, out_0, out_1, out_2
+):
+    nc = tc.nc
+    with ExitStack() as ctx:
+        keep = ctx.enter_context(tc.tile_pool(name="keep", bufs=1))
+        psum = ctx.enter_context(tc.psum_pool(name="psum", bufs=1))
+
+        def sbuf(shape, dtype, name, tag=None, bufs=1):
+            return keep.tile(shape, dtype, name=name, tag=tag or name, bufs=bufs, align_bytes=64)
+
+        def load_scale_rows(plane, scales, queue):
+            for q in range(4):
+                queue.dma_start(
+                    out=plane[32 * q : 32 * q + 4, :].bitcast(I32).rearrange("r (z c) -> r z c", z=scales.shape[0]),
+                    in_=scales[:, 4 * q : 4 * q + 4, :].bitcast(I32).rearrange("z r c -> r z c"),
+                )
+
+        list1 = sbuf([P, J // 16], U16, "list1")
+        list2 = sbuf([P, I // 16], U16, "list2")
+        xq_plane = sbuf([P, PASSES * T], U8, "xq_plane")
+        wa_plane = sbuf([P, PASSES * N], U8, "wa_plane")
+        wm_plane = sbuf([P, M], U8, "wm_plane")
+        xq_codes = [sbuf([P, T], U16, f"xq_codes{z}") for z in range(PASSES)]
+        wa_codes = sbuf([P, PASSES, N], U32, "wa_codes")
+        wm_codes = sbuf([P, M], U16, "wm_codes")
+        bias = sbuf([P, PACK], F32, "bias")
+        resid = [sbuf([P, T], F32, f"resid{t}") for t in range(PACK)]
+        pages = [sbuf([P, T], F32, f"page{u}") for u in range(2)]
+        ident = sbuf([P, P], F32, "ident")
+
+        for plane in (xq_plane, wa_plane, wm_plane):
+            nc.vector.memset(plane[:].bitcast(I32), 0)
+        make_identity(nc, ident[:])
+        for page in pages:
+            nc.vector.memset(page[:], 0.0)
+
+        nc.sync.dma_start(list1[:], offs)
+        nc.sync.dma_start(out=xq_codes[0][:].bitcast(I32), in_=xq_words[0].bitcast(I32))
+        nc.sync.dma_start(out=wa_codes[:].bitcast(I32), in_=wa_words.rearrange("z p n r -> p z (n r)").bitcast(I32))
+        load_scale_rows(xq_plane, xq_scales, nc.sync)
+        load_scale_rows(wa_plane, wa_scales, nc.sync)
+        nc.sync.dma_start(out=xq_codes[1][:].bitcast(I32), in_=xq_words[1].bitcast(I32))
+        load_scale_rows(wm_plane, wm_scales, nc.sync)
+        nc.sync.dma_start(out=wm_codes[:].bitcast(I32), in_=wm_words[0].bitcast(I32))
+        res_rows = res.rearrange("(p t) c -> p t c", t=PACK)
+        for t in range(PACK):
+            nc.sync.dma_start(out=resid[t][:], in_=res_rows[:, t, :])
+        nc.sync.dma_start(list2[:], offs2)
+        nc.sync.dma_start(out=bias[:], in_=b.rearrange("(p t) o -> p (t o)", t=PACK))
+
+        x_codes = [sbuf([P, J], U16, f"x_codes{z}") for z in range(PASSES)]
+        x_scales = [sbuf([P, J], U8, f"x_scales{z}") for z in range(PASSES)]
+        nc.vector.tensor_copy(x_codes[0][:], xq_codes[0][:].indirect(list1[:]))
+        for z in range(PASSES):
+            nc.vector.tensor_copy(x_scales[z][:], xq_plane[:, z * T : (z + 1) * T].indirect(list1[:]))
+        for blk in range(J // P):
+            nc.vector.tensor_copy(
+                x_codes[1][:, blk * P : (blk + 1) * P], xq_codes[1][:].indirect(list1[:, blk * P // 16 : (blk + 1) * P // 16])
+            )
+        product = sbuf([P, PACK, J], F32, "product", tag="product_then_picked")
+        for blk in range(J // P):
+            cols = slice(blk * P, (blk + 1) * P)
+            acc = psum.tile([P, N], F32, name=f"acc{blk}", tag="acc", bufs=2)
+            for z in range(PASSES):
+                nc.tensor.matmul_mx(
+                    out=acc[:],
+                    lhsT=x_codes[z][:, cols].bitcast(FP4X4),
+                    lhsT_scale=x_scales[z][:, cols],
+                    rhs=wa_codes[:, z, :].bitcast(FP8X4),
+                    rhs_scale=wa_plane[:, z * N : (z + 1) * N],
+                    start=(z == 0),
+                    stop=(z == PASSES - 1),
+                )
+            dealt = sbuf([P, PACK, P], F32, f"p_tokens{blk}")
+            nc.scalar.activation(dealt[:], acc[:].rearrange("j (q t) -> j t q", t=PACK), ACT.Copy)
+            turned = psum.tile([P, PACK, P], F32, name=f"turned{blk}", tag="turned", bufs=2)
+            for t in range(PACK):
+                nc.tensor.transpose(turned[:, t, :], dealt[:, t, :], ident[:])
+            nc.scalar.activation(product[:, :, cols], turned[:], ACT.Copy)
+
+        wm_dealt = sbuf([P, PACK, P], U16, "wm_dealt")
+        wm_dealt_plane = sbuf([P, PACK, P], U8, "wm_dealt_plane")
+        nc.vector.tensor_copy(wm_dealt[:], wm_codes[:].rearrange("p (q t) -> p t q", t=PACK))
+        nc.vector.tensor_copy(wm_dealt_plane[:], wm_plane[:].rearrange("p (q t) -> p t q", t=PACK))
+
+        updated = [sbuf([P, T], F32, f"updated{t}") for t in range(PACK)]
+        for t in range(PACK):
+            page = pages[t % 2]
+            cuts = ([0, P, 2 * P, 3 * P, J], [0, P, J], [0, J], [0, J])[t]
+            for lo, hi in zip(cuts, cuts[1:]):
+                nc.vector.tensor_copy(page[:].indirect(list1[:, lo // 16 : hi // 16]), product[:, t, lo:hi])
+            sums, up_tokens = [], []
+            banks = range(T // BANK - 1 if t == PACK - 1 else T // BANK)
+            for c in banks:
+                bank = psum.tile([P, BANK], F32, name=f"sum{t}{c}", tag=f"forth{c}")
+                terms = [(src, blk) for src in (resid[t], page) for blk in range(BANK // P)]
+                for n, (src, blk) in enumerate(terms):
+                    nc.tensor.matmul(
+                        bank[:, blk * P : (blk + 1) * P],
+                        lhsT=src[:, c * BANK + blk * P : c * BANK + (blk + 1) * P],
+                        rhs=ident[:],
+                        is_transpose=True,
+                        start=(n == 0),
+                        stop=(n == len(terms) - 1),
+                    )
+                sums.append(bank)
+            for c in banks:
+                held = sbuf([P, BANK], F32, f"up_tokens{t}{c}", tag=f"up_tokens{c}")
+                nc.scalar.activation(held[:], sums[c][:], ACT.Copy)
+                up_tokens.append(held)
+            for c in banks:
+                bank = psum.tile([P, BANK], F32, name=f"back{t}{c}", tag=f"back{c}")
+                for blk in range(BANK // P):
+                    nc.tensor.transpose(bank[:, blk * P : (blk + 1) * P], up_tokens[c][:, blk * P : (blk + 1) * P], ident[:])
+                nc.scalar.activation(updated[t][:, c * BANK : (c + 1) * BANK], bank[:], ACT.Copy)
+
+        picked = sbuf([P, PACK, I], BF16, "picked", tag="product_then_picked")
+        for t in range(PACK):
+            pieces = [(0, HALF), (HALF, I)] if t == PACK - 1 else [(0, I)]
+            for lo, hi in pieces:
+                nc.vector.tensor_copy(picked[:, t, lo:hi], updated[t][:].indirect(list2[:, lo // 16 : hi // 16]))
+            if t == 0:
+                last = PACK - 1
+                nc.vector.tensor_tensor(updated[last][:, BANK:], resid[last][:, BANK:], pages[last % 2][:, BANK:], ALU.add)
+
+        halves = range(I // HALF)
+        us_bf = [sbuf([P, HALF, PACK], BF16, f"us_bf{h}") for h in halves]
+        us_codes = [sbuf([P, HALF], U32, f"us_codes{h}") for h in halves]
+        us_scales = [sbuf([P, HALF], U8, f"us_scales{h}") for h in halves]
+        for h in halves:
+            src = picked[:, :, h * HALF : (h + 1) * HALF].rearrange("p t c -> p c t")
+            if h == 0:
+                nc.scalar.copy(us_bf[h][:], src)
+            else:
+                nc.vector.tensor_copy(us_bf[h][:], src)
+        for h in halves:
+            nc.vector.quantize_mx(
+                out=us_codes[h][:].bitcast(FP8X4), scales=us_scales[h][:], in_=us_bf[h][:].rearrange("p c t -> p (c t)")
+            )
+
+        out_rows = out_0.rearrange("(p t) c -> p t c", t=PACK)
+        out_words = out_1[0].rearrange("p c r -> p (c r)").bitcast(I32)
+        y_plane = sbuf([P, I], U8, "y_plane")
+        for h in halves:
+            cols = slice(h * HALF, (h + 1) * HALF)
+            y = sbuf([P, PACK, HALF], F32, f"y{h}")
+            for pair in range(2):
+                z_bank = psum.tile([P, 2, HALF], F32, name=f"z{h}{pair}", tag=("acc", "turned")[pair], bufs=2)
+                for u in range(2):
+                    t = 2 * pair + u
+                    nc.tensor.matmul_mx(
+                        out=z_bank[:, u, :],
+                        lhsT=wm_dealt[:, t, :].bitcast(FP4X4),
+                        lhsT_scale=wm_dealt_plane[:, t, :],
+                        rhs=us_codes[h][:].bitcast(FP8X4),
+                        rhs_scale=us_scales[h][:],
+                        start=True,
+                        stop=True,
+                    )
+                for u in range(2):
+                    t = 2 * pair + u
+                    if pair == 0:
+                        nc.scalar.activation(y[:, t, :], z_bank[:, u, :], ACT.Relu, bias=bias[:, t : t + 1])
+                    else:
+                        nc.vector.tensor_scalar(y[:, t, :], z_bank[:, u, :], bias[:, t : t + 1], 0.0, ALU.add, ALU.max)
+            nc.sync.dma_start(out=out_rows[:, :, cols], in_=y[:])
+            y_bf = sbuf([P, HALF, PACK], BF16, f"y_bf{h}")
+            nc.vector.tensor_copy(y_bf[:], y[:].rearrange("p t c -> p c t"))
+            y_codes = sbuf([P, HALF], U32, f"y_codes{h}")
+            nc.vector.quantize_mx(
+                out=y_codes[:].bitcast(FP8X4), scales=y_plane[:, cols], in_=y_bf[:].rearrange("p c t -> p (c t)")
+            )
+            nc.sync.dma_start(out=out_words[:, cols], in_=y_codes[:].bitcast(I32))
+        for q in range(4):
+            queue = (nc.scalar, nc.sync)[q % 2]
+            queue.dma_start(
+                out=out_2[0, 4 * q : 4 * q + 4, :].bitcast(I32), in_=y_plane[32 * q : 32 * q + 4, :].bitcast(I32)
+            )

@@ -22,6 +22,7 @@ PACK = 4
 PASSES = K // (P * PACK)
 BANK = 512
 HALF = 256
+ON_VECTOR = ((1, 2), (0, 1))
 
 
 def tile_list_second_reads_updated_page_pl_kernel(
@@ -42,6 +43,9 @@ def tile_list_second_reads_updated_page_pl_kernel(
                     in_=scales[:, 4 * q : 4 * q + 4, :].bitcast(I32).rearrange("z r c -> r z c"),
                 )
 
+        def interleave(copy, words, planes):
+            copy(words.rearrange("p (c i) t -> p c t i", i=4), planes.rearrange("p t (c i) -> p c t i", i=4))
+
         list1 = sbuf([P, J // 16], U16, "list1")
         list2 = sbuf([P, I // 16], U16, "list2")
         xq_plane = sbuf([P, PASSES * T], U8, "xq_plane")
@@ -58,13 +62,13 @@ def tile_list_second_reads_updated_page_pl_kernel(
         for plane in (xq_plane, wa_plane, wm_plane):
             nc.vector.memset(plane[:].bitcast(I32), 0)
         make_identity(nc, ident[:])
-        for page in pages:
-            nc.vector.memset(page[:], 0.0)
+        nc.vector.memset(pages[0][:], 0.0)
+        nc.gpsimd.memset(pages[1][:], 0.0)
 
         nc.sync.dma_start(list1[:], offs)
         nc.sync.dma_start(out=xq_codes[0][:].bitcast(I32), in_=xq_words[0].bitcast(I32))
-        nc.sync.dma_start(out=wa_codes[:].bitcast(I32), in_=wa_words.rearrange("z p n r -> p z (n r)").bitcast(I32))
         load_scale_rows(xq_plane, xq_scales, nc.sync)
+        nc.sync.dma_start(out=wa_codes[:].bitcast(I32), in_=wa_words.rearrange("z p n r -> p z (n r)").bitcast(I32))
         load_scale_rows(wa_plane, wa_scales, nc.sync)
         nc.sync.dma_start(out=xq_codes[1][:].bitcast(I32), in_=xq_words[1].bitcast(I32))
         load_scale_rows(wm_plane, wm_scales, nc.sync)
@@ -75,45 +79,47 @@ def tile_list_second_reads_updated_page_pl_kernel(
         nc.sync.dma_start(list2[:], offs2)
         nc.sync.dma_start(out=bias[:], in_=b.rearrange("(p t) o -> p (t o)", t=PACK))
 
+        def deal(name, dtype, packed, passes):
+            dealt = sbuf([P, passes, PACK, P], dtype, name)
+            nc.vector.tensor_copy(
+                dealt[:].rearrange("p z t q -> p z q t"), packed.rearrange("p (z q t) -> p z q t", z=passes, t=PACK)
+            )
+            return dealt
+
         x_codes = [sbuf([P, J], U16, f"x_codes{z}") for z in range(PASSES)]
         x_scales = [sbuf([P, J], U8, f"x_scales{z}") for z in range(PASSES)]
         nc.vector.tensor_copy(x_codes[0][:], xq_codes[0][:].indirect(list1[:]))
         for z in range(PASSES):
             nc.vector.tensor_copy(x_scales[z][:], xq_plane[:, z * T : (z + 1) * T].indirect(list1[:]))
-        for blk in range(J // P):
-            nc.vector.tensor_copy(
-                x_codes[1][:, blk * P : (blk + 1) * P], xq_codes[1][:].indirect(list1[:, blk * P // 16 : (blk + 1) * P // 16])
-            )
-        product = sbuf([P, PACK, J], F32, "product", tag="product_then_picked")
-        for blk in range(J // P):
-            cols = slice(blk * P, (blk + 1) * P)
-            acc = psum.tile([P, N], F32, name=f"acc{blk}", tag="acc", bufs=2)
-            for z in range(PASSES):
-                nc.tensor.matmul_mx(
-                    out=acc[:],
-                    lhsT=x_codes[z][:, cols].bitcast(FP4X4),
-                    lhsT_scale=x_scales[z][:, cols],
-                    rhs=wa_codes[:, z, :].bitcast(FP8X4),
-                    rhs_scale=wa_plane[:, z * N : (z + 1) * N],
-                    start=(z == 0),
-                    stop=(z == PASSES - 1),
-                )
-            dealt = sbuf([P, PACK, P], F32, f"p_tokens{blk}")
-            nc.scalar.activation(dealt[:], acc[:].rearrange("j (q t) -> j t q", t=PACK), ACT.Copy)
-            turned = psum.tile([P, PACK, P], F32, name=f"turned{blk}", tag="turned", bufs=2)
-            for t in range(PACK):
-                nc.tensor.transpose(turned[:, t, :], dealt[:, t, :], ident[:])
-            nc.scalar.activation(product[:, :, cols], turned[:], ACT.Copy)
+        wa_dealt = deal("wa_dealt", U32, wa_codes[:].rearrange("p z n -> p (z n)"), PASSES)
+        wa_dealt_plane = deal("wa_dealt_plane", U8, wa_plane[:], PASSES)
+        for lo in (0, HALF):
+            nc.vector.tensor_copy(x_codes[1][:, lo : lo + HALF], xq_codes[1][:].indirect(list1[:, lo // 16 : (lo + HALF) // 16]))
+        wm_dealt = deal("wm_dealt", U16, wm_codes[:], 1)
+        wm_dealt_plane = deal("wm_dealt_plane", U8, wm_plane[:], 1)
 
-        wm_dealt = sbuf([P, PACK, P], U16, "wm_dealt")
-        wm_dealt_plane = sbuf([P, PACK, P], U8, "wm_dealt_plane")
-        nc.vector.tensor_copy(wm_dealt[:], wm_codes[:].rearrange("p (q t) -> p t q", t=PACK))
-        nc.vector.tensor_copy(wm_dealt_plane[:], wm_plane[:].rearrange("p (q t) -> p t q", t=PACK))
+        product = sbuf([P, PACK, J], F32, "product", tag="product_then_picked")
+        pieces = [(0, 0, HALF, P, "acc"), (0, HALF, J, P, "forth1"), (1, 0, J, J, "forth0"), (2, 0, J, J, "acc"), (3, 0, J, J, "acc")]
+        for t, lo, hi, width, tag in pieces:
+            acc = psum.tile([P, hi - lo], F32, name=f"acc{t}_{lo}", tag=tag)
+            for c in range(lo, hi, width):
+                cols = slice(c, c + width)
+                for z in range(PASSES):
+                    nc.tensor.matmul_mx(
+                        out=acc[:, c - lo : c - lo + width],
+                        lhsT=wa_dealt[:, z, t, :].bitcast(FP8X4),
+                        lhsT_scale=wa_dealt_plane[:, z, t, :],
+                        rhs=x_codes[z][:, cols].bitcast(FP4X4),
+                        rhs_scale=x_scales[z][:, cols],
+                        start=(z == 0),
+                        stop=(z == PASSES - 1),
+                    )
+            nc.scalar.activation(product[:, t, lo:hi], acc[:], ACT.Copy)
 
         updated = [sbuf([P, T], F32, f"updated{t}") for t in range(PACK)]
         for t in range(PACK):
             page = pages[t % 2]
-            cuts = ([0, P, 2 * P, 3 * P, J], [0, P, J], [0, J], [0, J])[t]
+            cuts = [0, HALF, J] if t == 0 else [0, J]
             for lo, hi in zip(cuts, cuts[1:]):
                 nc.vector.tensor_copy(page[:].indirect(list1[:, lo // 16 : hi // 16]), product[:, t, lo:hi])
             sums, up_tokens = [], []
@@ -141,63 +147,61 @@ def tile_list_second_reads_updated_page_pl_kernel(
                     nc.tensor.transpose(bank[:, blk * P : (blk + 1) * P], up_tokens[c][:, blk * P : (blk + 1) * P], ident[:])
                 nc.scalar.activation(updated[t][:, c * BANK : (c + 1) * BANK], bank[:], ACT.Copy)
 
+        chunks = [(0, HALF), (HALF, HALF + P), (HALF + P, I)]
+        last = PACK - 1
         picked = sbuf([P, PACK, I], BF16, "picked", tag="product_then_picked")
         for t in range(PACK):
-            pieces = [(0, HALF), (HALF, I)] if t == PACK - 1 else [(0, I)]
-            for lo, hi in pieces:
+            for lo, hi in chunks if t == last else [(0, I)]:
                 nc.vector.tensor_copy(picked[:, t, lo:hi], updated[t][:].indirect(list2[:, lo // 16 : hi // 16]))
             if t == 0:
-                last = PACK - 1
                 nc.vector.tensor_tensor(updated[last][:, BANK:], resid[last][:, BANK:], pages[last % 2][:, BANK:], ALU.add)
 
-        halves = range(I // HALF)
-        us_bf = [sbuf([P, HALF, PACK], BF16, f"us_bf{h}") for h in halves]
-        us_codes = [sbuf([P, HALF], U32, f"us_codes{h}") for h in halves]
-        us_scales = [sbuf([P, HALF], U8, f"us_scales{h}") for h in halves]
-        for h in halves:
-            src = picked[:, :, h * HALF : (h + 1) * HALF].rearrange("p t c -> p c t")
-            if h == 0:
-                nc.scalar.copy(us_bf[h][:], src)
-            else:
-                nc.vector.tensor_copy(us_bf[h][:], src)
-        for h in halves:
+        us_bf = [sbuf([P, hi - lo, PACK], BF16, f"us_bf{lo}") for lo, hi in chunks]
+        us_codes = [sbuf([P, hi - lo], U32, f"us_codes{lo}") for lo, hi in chunks]
+        us_scales = [sbuf([P, hi - lo], U8, f"us_scales{lo}") for lo, hi in chunks]
+        for h, (lo, hi) in enumerate(chunks):
+            interleave(nc.scalar.copy if h == 0 else nc.vector.tensor_copy, us_bf[h][:], picked[:, :, lo:hi])
+        order = (1, 0, 2)
+        for h in order:
             nc.vector.quantize_mx(
                 out=us_codes[h][:].bitcast(FP8X4), scales=us_scales[h][:], in_=us_bf[h][:].rearrange("p c t -> p (c t)")
             )
 
         out_rows = out_0.rearrange("(p t) c -> p t c", t=PACK)
         out_words = out_1[0].rearrange("p c r -> p (c r)").bitcast(I32)
+        z_tags = ["spare0", "spare1", "spare2", "acc", "forth0", "forth1", "back0", "back1"]
         y_plane = sbuf([P, I], U8, "y_plane")
-        for h in halves:
-            cols = slice(h * HALF, (h + 1) * HALF)
-            y = sbuf([P, PACK, HALF], F32, f"y{h}")
-            for pair in range(2):
-                z_bank = psum.tile([P, 2, HALF], F32, name=f"z{h}{pair}", tag=("acc", "turned")[pair], bufs=2)
-                for u in range(2):
-                    t = 2 * pair + u
+        for h in order:
+            lo, hi = chunks[h]
+            width = hi - lo
+            y = sbuf([P, PACK, width], F32, f"y{h}")
+            share = HALF // width
+            for t0 in range(0, PACK, share):
+                z_bank = psum.tile([P, share, width], F32, name=f"z{h}{t0}", tag=z_tags.pop(0))
+                for u in range(share):
                     nc.tensor.matmul_mx(
                         out=z_bank[:, u, :],
-                        lhsT=wm_dealt[:, t, :].bitcast(FP4X4),
-                        lhsT_scale=wm_dealt_plane[:, t, :],
+                        lhsT=wm_dealt[:, 0, t0 + u, :].bitcast(FP4X4),
+                        lhsT_scale=wm_dealt_plane[:, 0, t0 + u, :],
                         rhs=us_codes[h][:].bitcast(FP8X4),
                         rhs_scale=us_scales[h][:],
                         start=True,
                         stop=True,
                     )
-                for u in range(2):
-                    t = 2 * pair + u
-                    if pair == 0:
-                        nc.scalar.activation(y[:, t, :], z_bank[:, u, :], ACT.Relu, bias=bias[:, t : t + 1])
-                    else:
+                for u in range(share):
+                    t = t0 + u
+                    if (h, t0) in ON_VECTOR:
                         nc.vector.tensor_scalar(y[:, t, :], z_bank[:, u, :], bias[:, t : t + 1], 0.0, ALU.add, ALU.max)
-            nc.sync.dma_start(out=out_rows[:, :, cols], in_=y[:])
-            y_bf = sbuf([P, HALF, PACK], BF16, f"y_bf{h}")
-            nc.vector.tensor_copy(y_bf[:], y[:].rearrange("p t c -> p c t"))
-            y_codes = sbuf([P, HALF], U32, f"y_codes{h}")
+                    else:
+                        nc.scalar.activation(y[:, t, :], z_bank[:, u, :], ACT.Relu, bias=bias[:, t : t + 1])
+            nc.sync.dma_start(out=out_rows[:, :, lo:hi], in_=y[:])
+            y_bf = sbuf([P, width, PACK], BF16, f"y_bf{h}")
+            interleave(nc.vector.tensor_copy, y_bf[:], y[:])
+            y_codes = sbuf([P, width], U32, f"y_codes{h}")
             nc.vector.quantize_mx(
-                out=y_codes[:].bitcast(FP8X4), scales=y_plane[:, cols], in_=y_bf[:].rearrange("p c t -> p (c t)")
+                out=y_codes[:].bitcast(FP8X4), scales=y_plane[:, lo:hi], in_=y_bf[:].rearrange("p c t -> p (c t)")
             )
-            nc.sync.dma_start(out=out_words[:, cols], in_=y_codes[:].bitcast(I32))
+            nc.sync.dma_start(out=out_words[:, lo:hi], in_=y_codes[:].bitcast(I32))
         for q in range(4):
             queue = (nc.scalar, nc.sync)[q % 2]
             queue.dma_start(

@@ -22,6 +22,7 @@ PACK = 4
 PASSES = K // (P * PACK)
 BANK = 512
 HALF = 256
+VECTOR_COLUMNS = 256
 ON_VECTOR = ((1, 2), (0, 1))
 
 
@@ -66,7 +67,7 @@ def tile_list_second_reads_updated_page_pl_kernel(
         nc.gpsimd.memset(pages[1][:], 0.0)
 
         nc.sync.dma_start(list1[:], offs)
-        nc.sync.dma_start(out=xq_codes[0][:].bitcast(I32), in_=xq_words[0].bitcast(I32))
+        nc.scalar.dma_start(out=xq_codes[0][:].bitcast(I32), in_=xq_words[0].bitcast(I32))
         load_scale_rows(xq_plane, xq_scales, nc.sync)
         nc.sync.dma_start(out=wa_codes[:].bitcast(I32), in_=wa_words.rearrange("z p n r -> p z (n r)").bitcast(I32))
         load_scale_rows(wa_plane, wa_scales, nc.sync)
@@ -99,7 +100,7 @@ def tile_list_second_reads_updated_page_pl_kernel(
         wm_dealt_plane = deal("wm_dealt_plane", U8, wm_plane[:], 1)
 
         product = sbuf([P, PACK, J], F32, "product", tag="product_then_picked")
-        pieces = [(0, 0, HALF, P, "acc"), (0, HALF, J, P, "forth1"), (1, 0, J, J, "forth0"), (2, 0, J, J, "acc"), (3, 0, J, J, "acc")]
+        pieces = [(0, 0, P, P, "acc"), (0, P, HALF, P, "spare0"), (0, HALF, J, P, "forth1"), (1, 0, J, J, "forth0"), (2, 0, J, J, "acc"), (3, 0, J, J, "acc")]
         for t, lo, hi, width, tag in pieces:
             acc = psum.tile([P, hi - lo], F32, name=f"acc{t}_{lo}", tag=tag)
             for c in range(lo, hi, width):
@@ -119,33 +120,33 @@ def tile_list_second_reads_updated_page_pl_kernel(
         updated = [sbuf([P, T], F32, f"updated{t}") for t in range(PACK)]
         for t in range(PACK):
             page = pages[t % 2]
-            cuts = [0, HALF, J] if t == 0 else [0, J]
+            cuts = [0, P, HALF, J] if t == 0 else [0, J]
             for lo, hi in zip(cuts, cuts[1:]):
                 nc.vector.tensor_copy(page[:].indirect(list1[:, lo // 16 : hi // 16]), product[:, t, lo:hi])
             sums, up_tokens = [], []
-            banks = range(T // BANK - 1 if t == PACK - 1 else T // BANK)
-            for c in banks:
-                bank = psum.tile([P, BANK], F32, name=f"sum{t}{c}", tag=f"forth{c}")
-                terms = [(src, blk) for src in (resid[t], page) for blk in range(BANK // P)]
-                for n, (src, blk) in enumerate(terms):
+            spans = [(0, BANK), (BANK, T - VECTOR_COLUMNS if t == PACK - 1 else T)]
+            for c, (lo, hi) in enumerate(spans):
+                bank = psum.tile([P, hi - lo], F32, name=f"sum{t}{c}", tag=f"forth{c}")
+                terms = [(src, col) for src in (resid[t], page) for col in range(lo, hi, P)]
+                for n, (src, col) in enumerate(terms):
                     nc.tensor.matmul(
-                        bank[:, blk * P : (blk + 1) * P],
-                        lhsT=src[:, c * BANK + blk * P : c * BANK + (blk + 1) * P],
+                        bank[:, col - lo : col - lo + P],
+                        lhsT=src[:, col : col + P],
                         rhs=ident[:],
                         is_transpose=True,
                         start=(n == 0),
                         stop=(n == len(terms) - 1),
                     )
                 sums.append(bank)
-            for c in banks:
-                held = sbuf([P, BANK], F32, f"up_tokens{t}{c}", tag=f"up_tokens{c}")
+            for c, (lo, hi) in enumerate(spans):
+                held = sbuf([P, hi - lo], F32, f"up_tokens{t}{c}", tag=f"up_tokens{c}")
                 nc.scalar.activation(held[:], sums[c][:], ACT.Copy)
                 up_tokens.append(held)
-            for c in banks:
-                bank = psum.tile([P, BANK], F32, name=f"back{t}{c}", tag=f"back{c}")
-                for blk in range(BANK // P):
-                    nc.tensor.transpose(bank[:, blk * P : (blk + 1) * P], up_tokens[c][:, blk * P : (blk + 1) * P], ident[:])
-                nc.scalar.activation(updated[t][:, c * BANK : (c + 1) * BANK], bank[:], ACT.Copy)
+            for c, (lo, hi) in enumerate(spans):
+                bank = psum.tile([P, hi - lo], F32, name=f"back{t}{c}", tag=f"back{c}")
+                for col in range(0, hi - lo, P):
+                    nc.tensor.transpose(bank[:, col : col + P], up_tokens[c][:, col : col + P], ident[:])
+                nc.scalar.activation(updated[t][:, lo:hi], bank[:], ACT.Copy)
 
         chunks = [(0, HALF), (HALF, HALF + P), (HALF + P, I)]
         last = PACK - 1
@@ -154,7 +155,8 @@ def tile_list_second_reads_updated_page_pl_kernel(
             for lo, hi in chunks if t == last else [(0, I)]:
                 nc.vector.tensor_copy(picked[:, t, lo:hi], updated[t][:].indirect(list2[:, lo // 16 : hi // 16]))
             if t == 0:
-                nc.vector.tensor_tensor(updated[last][:, BANK:], resid[last][:, BANK:], pages[last % 2][:, BANK:], ALU.add)
+                own = slice(T - VECTOR_COLUMNS, T)
+                nc.vector.tensor_tensor(updated[last][:, own], resid[last][:, own], pages[last % 2][:, own], ALU.add)
 
         us_bf = [sbuf([P, hi - lo, PACK], BF16, f"us_bf{lo}") for lo, hi in chunks]
         us_codes = [sbuf([P, hi - lo], U32, f"us_codes{lo}") for lo, hi in chunks]

from contextlib import ExitStack

import concourse.mybir as mybir
from concourse.masks import make_identity

K, T, J, I, N, M = 1024, 1024, 512, 512, 512, 512
FLOPS = 2 * K * N * J + 2 * N * M * I

F32 = mybir.dt.float32
BF16 = mybir.dt.bfloat16
I32 = mybir.dt.int32
U32 = mybir.dt.uint32
U16 = mybir.dt.uint16
U8 = mybir.dt.uint8
FP8X4 = mybir.dt.float8_e4m3fn_x4
FP4X4 = mybir.dt.float4_e2m1fn_x4
ACT = mybir.ActivationFunctionType
ALU = mybir.AluOpType

P = 128
PACK = 4
PASSES = K // (P * PACK)
BANK = 512
HALF = 256
VECTOR_COLUMNS = 256
ON_VECTOR = ((1, 2), (0, 1))


def tile_list_second_reads_updated_page_pl_kernel(
    tc, xq_words, xq_scales, wa_words, wa_scales, res, wm_words, wm_scales, b, offs, offs2, out_0, out_1, out_2
):
    nc = tc.nc
    with ExitStack() as ctx:
        keep = ctx.enter_context(tc.tile_pool(name="keep", bufs=1))
        psum = ctx.enter_context(tc.psum_pool(name="psum", bufs=1))

        def sbuf(shape, dtype, name, tag=None, bufs=1):
            return keep.tile(shape, dtype, name=name, tag=tag or name, bufs=bufs, align_bytes=64)

        def load_scale_rows(plane, scales, queue):
            for q in range(4):
                queue.dma_start(
                    out=plane[32 * q : 32 * q + 4, :].bitcast(I32).rearrange("r (z c) -> r z c", z=scales.shape[0]),
                    in_=scales[:, 4 * q : 4 * q + 4, :].bitcast(I32).rearrange("z r c -> r z c"),
                )

        def interleave(copy, words, planes):
            copy(words.rearrange("p (c i) t -> p c t i", i=4), planes.rearrange("p t (c i) -> p c t i", i=4))

        list1 = sbuf([P, J // 16], U16, "list1")
        list2 = sbuf([P, I // 16], U16, "list2")
        xq_plane = sbuf([P, PASSES * T], U8, "xq_plane")
        wa_plane = sbuf([P, PASSES * N], U8, "wa_plane")
        wm_plane = sbuf([P, M], U8, "wm_plane")
        xq_codes = [sbuf([P, T], U16, f"xq_codes{z}") for z in range(PASSES)]
        wa_codes = sbuf([P, PASSES, N], U32, "wa_codes")
        wm_codes = sbuf([P, M], U16, "wm_codes")
        bias = sbuf([P, PACK], F32, "bias")
        resid = [sbuf([P, T], F32, f"resid{t}") for t in range(PACK)]
        pages = [sbuf([P, T], F32, f"page{u}") for u in range(2)]
        ident = sbuf([P, P], F32, "ident")

        for plane in (xq_plane, wa_plane, wm_plane):
            nc.vector.memset(plane[:].bitcast(I32), 0)
        make_identity(nc, ident[:])
        nc.vector.memset(pages[0][:], 0.0)
        nc.gpsimd.memset(pages[1][:], 0.0)

        nc.sync.dma_start(list1[:], offs)
        nc.scalar.dma_start(out=xq_codes[0][:].bitcast(I32), in_=xq_words[0].bitcast(I32))
        load_scale_rows(xq_plane, xq_scales, nc.sync)
        nc.sync.dma_start(out=wa_codes[:].bitcast(I32), in_=wa_words.rearrange("z p n r -> p z (n r)").bitcast(I32))
        load_scale_rows(wa_plane, wa_scales, nc.sync)
        nc.sync.dma_start(out=xq_codes[1][:].bitcast(I32), in_=xq_words[1].bitcast(I32))
        load_scale_rows(wm_plane, wm_scales, nc.sync)
        nc.sync.dma_start(out=wm_codes[:].bitcast(I32), in_=wm_words[0].bitcast(I32))
        res_rows = res.rearrange("(p t) c -> p t c", t=PACK)
        for t in range(PACK):
            nc.sync.dma_start(out=resid[t][:], in_=res_rows[:, t, :])
        nc.sync.dma_start(list2[:], offs2)
        nc.sync.dma_start(out=bias[:], in_=b.rearrange("(p t) o -> p (t o)", t=PACK))

        def deal(name, dtype, packed, passes):
            dealt = sbuf([P, passes, PACK, P], dtype, name)
            nc.vector.tensor_copy(
                dealt[:].rearrange("p z t q -> p z q t"), packed.rearrange("p (z q t) -> p z q t", z=passes, t=PACK)
            )
            return dealt

        x_codes = [sbuf([P, J], U16, f"x_codes{z}") for z in range(PASSES)]
        x_scales = [sbuf([P, J], U8, f"x_scales{z}") for z in range(PASSES)]
        nc.vector.tensor_copy(x_codes[0][:], xq_codes[0][:].indirect(list1[:]))
        for z in range(PASSES):
            nc.vector.tensor_copy(x_scales[z][:], xq_plane[:, z * T : (z + 1) * T].indirect(list1[:]))
        wa_dealt = deal("wa_dealt", U32, wa_codes[:].rearrange("p z n -> p (z n)"), PASSES)
        wa_dealt_plane = deal("wa_dealt_plane", U8, wa_plane[:], PASSES)
        for lo in (0, HALF):
            nc.vector.tensor_copy(x_codes[1][:, lo : lo + HALF], xq_codes[1][:].indirect(list1[:, lo // 16 : (lo + HALF) // 16]))
        wm_dealt = deal("wm_dealt", U16, wm_codes[:], 1)
        wm_dealt_plane = deal("wm_dealt_plane", U8, wm_plane[:], 1)

        product = sbuf([P, PACK, J], F32, "product", tag="product_then_picked")
        pieces = [(0, 0, P, P, "acc"), (0, P, HALF, P, "spare0"), (0, HALF, J, P, "forth1"), (1, 0, J, J, "forth0"), (2, 0, J, J, "acc"), (3, 0, J, J, "acc")]
        for t, lo, hi, width, tag in pieces:
            acc = psum.tile([P, hi - lo], F32, name=f"acc{t}_{lo}", tag=tag)
            for c in range(lo, hi, width):
                cols = slice(c, c + width)
                for z in range(PASSES):
                    nc.tensor.matmul_mx(
                        out=acc[:, c - lo : c - lo + width],
                        lhsT=wa_dealt[:, z, t, :].bitcast(FP8X4),
                        lhsT_scale=wa_dealt_plane[:, z, t, :],
                        rhs=x_codes[z][:, cols].bitcast(FP4X4),
                        rhs_scale=x_scales[z][:, cols],
                        start=(z == 0),
                        stop=(z == PASSES - 1),
                    )
            nc.scalar.activation(product[:, t, lo:hi], acc[:], ACT.Copy)

        updated = [sbuf([P, T], F32, f"updated{t}") for t in range(PACK)]
        for t in range(PACK):
            page = pages[t % 2]
            cuts = [0, P, HALF, J] if t == 0 else [0, J]
            for lo, hi in zip(cuts, cuts[1:]):
                nc.vector.tensor_copy(page[:].indirect(list1[:, lo // 16 : hi // 16]), product[:, t, lo:hi])
            sums, up_tokens = [], []
            spans = [(0, BANK), (BANK, T - VECTOR_COLUMNS if t == PACK - 1 else T)]
            for c, (lo, hi) in enumerate(spans):
                bank = psum.tile([P, hi - lo], F32, name=f"sum{t}{c}", tag=f"forth{c}")
                terms = [(src, col) for src in (resid[t], page) for col in range(lo, hi, P)]
                for n, (src, col) in enumerate(terms):
                    nc.tensor.matmul(
                        bank[:, col - lo : col - lo + P],
                        lhsT=src[:, col : col + P],
                        rhs=ident[:],
                        is_transpose=True,
                        start=(n == 0),
                        stop=(n == len(terms) - 1),
                    )
                sums.append(bank)
            for c, (lo, hi) in enumerate(spans):
                held = sbuf([P, hi - lo], F32, f"up_tokens{t}{c}", tag=f"up_tokens{c}")
                nc.scalar.activation(held[:], sums[c][:], ACT.Copy)
                up_tokens.append(held)
            for c, (lo, hi) in enumerate(spans):
                bank = psum.tile([P, hi - lo], F32, name=f"back{t}{c}", tag=f"back{c}")
                for col in range(0, hi - lo, P):
                    nc.tensor.transpose(bank[:, col : col + P], up_tokens[c][:, col : col + P], ident[:])
                nc.scalar.activation(updated[t][:, lo:hi], bank[:], ACT.Copy)

        chunks = [(0, HALF), (HALF, HALF + P), (HALF + P, I)]
        last = PACK - 1
        picked = sbuf([P, PACK, I], BF16, "picked", tag="product_then_picked")
        for t in range(PACK):
            for lo, hi in chunks if t == last else [(0, I)]:
                nc.vector.tensor_copy(picked[:, t, lo:hi], updated[t][:].indirect(list2[:, lo // 16 : hi // 16]))
            if t == 0:
                own = slice(T - VECTOR_COLUMNS, T)
                nc.vector.tensor_tensor(updated[last][:, own], resid[last][:, own], pages[last % 2][:, own], ALU.add)

        us_bf = [sbuf([P, hi - lo, PACK], BF16, f"us_bf{lo}") for lo, hi in chunks]
        us_codes = [sbuf([P, hi - lo], U32, f"us_codes{lo}") for lo, hi in chunks]
        us_scales = [sbuf([P, hi - lo], U8, f"us_scales{lo}") for lo, hi in chunks]
        for h, (lo, hi) in enumerate(chunks):
            interleave(nc.scalar.copy if h == 0 else nc.vector.tensor_copy, us_bf[h][:], picked[:, :, lo:hi])
        order = (1, 0, 2)
        for h in order:
            nc.vector.quantize_mx(
                out=us_codes[h][:].bitcast(FP8X4), scales=us_scales[h][:], in_=us_bf[h][:].rearrange("p c t -> p (c t)")
            )

        out_rows = out_0.rearrange("(p t) c -> p t c", t=PACK)
        out_words = out_1[0].rearrange("p c r -> p (c r)").bitcast(I32)
        z_tags = ["spare0", "spare1", "spare2", "acc", "forth0", "forth1", "back0", "back1"]
        y_plane = sbuf([P, I], U8, "y_plane")
        for h in order:
            lo, hi = chunks[h]
            width = hi - lo
            y = sbuf([P, PACK, width], F32, f"y{h}")
            share = HALF // width
            for t0 in range(0, PACK, share):
                z_bank = psum.tile([P, share, width], F32, name=f"z{h}{t0}", tag=z_tags.pop(0))
                for u in range(share):
                    nc.tensor.matmul_mx(
                        out=z_bank[:, u, :],
                        lhsT=wm_dealt[:, 0, t0 + u, :].bitcast(FP4X4),
                        lhsT_scale=wm_dealt_plane[:, 0, t0 + u, :],
                        rhs=us_codes[h][:].bitcast(FP8X4),
                        rhs_scale=us_scales[h][:],
                        start=True,
                        stop=True,
                    )
                for u in range(share):
                    t = t0 + u
                    if (h, t0) in ON_VECTOR:
                        nc.vector.tensor_scalar(y[:, t, :], z_bank[:, u, :], bias[:, t : t + 1], 0.0, ALU.add, ALU.max)
                    else:
                        nc.scalar.activation(y[:, t, :], z_bank[:, u, :], ACT.Relu, bias=bias[:, t : t + 1])
            nc.sync.dma_start(out=out_rows[:, :, lo:hi], in_=y[:])
            y_bf = sbuf([P, width, PACK], BF16, f"y_bf{h}")
            interleave(nc.vector.tensor_copy, y_bf[:], y[:])
            y_codes = sbuf([P, width], U32, f"y_codes{h}")
            nc.vector.quantize_mx(
                out=y_codes[:].bitcast(FP8X4), scales=y_plane[:, lo:hi], in_=y_bf[:].rearrange("p c t -> p (c t)")
            )
            nc.sync.dma_start(out=out_words[:, lo:hi], in_=y_codes[:].bitcast(I32))
        for q in range(4):
            queue = (nc.scalar, nc.sync)[q % 2]
            queue.dma_start(
                out=out_2[0, 4 * q : 4 * q + 4, :].bitcast(I32), in_=y_plane[32 * q : 32 * q + 4, :].bitcast(I32)
            )
